import numpy as np
import ml_dtypes


def mxq(x, axis, fmt="e4m3"):
    dtype, down = {"e4m3": (ml_dtypes.float8_e4m3fn, 7), "e5m2": (ml_dtypes.float8_e5m2, 14)}[fmt]
    v = np.moveaxis(np.asarray(x, np.float32).astype(ml_dtypes.bfloat16).astype(np.float64), axis, -1)
    blocks = v.reshape(v.shape[:-1] + (-1, 32))
    amax = np.abs(blocks).max(-1, keepdims=True)
    byte = np.maximum(np.where(amax > 0, np.frexp(amax)[1] - 1 + 127, 0) - down, 1)
    scale = np.exp2(byte - 127.0)
    codes = (blocks / scale).astype(np.float32).astype(dtype).astype(np.float64)
    return np.moveaxis((codes * scale).reshape(v.shape), -1, axis)


WIDE = False


def mx_kscale(k):
    if not WIDE:
        return np.ones(k)
    levels = np.array([10, -10, 5, -5, 0])
    if k % 512:
        return np.exp2(np.random.permutation(np.resize(levels, k // 32))).repeat(32)
    a = np.empty((k // 512, 16))
    for p in range(k // 512):
        a[p, :8] = np.random.permutation(np.resize(levels, 8))
        for g in range(8):
            far = levels[np.abs(levels - a[p, g]) >= 10]
            a[p, g + 8] = far[np.random.randint(len(far))]
    return np.exp2(a.ravel()).repeat(32)


def f64(x):
    return np.asarray(x).astype(np.float64)


def striped(idx):
    return np.tile(np.asarray(idx).reshape(-1, 16).T, (8, 1)).astype(np.uint16)


def unstriped(offs):
    return offs[:16].T.reshape(-1).astype(np.int64)


B, N, T, D, DV, NQ = 1, 512, 1024, 512, 512, 128
NEW = 256


def setup_inputs():
    n = np.random.standard_normal
    idx = np.random.permutation(T)[:B * N]
    s = mx_kscale(D)[:, None]
    u = np.ones(T)
    u[idx] = mx_kscale(B * N)
    r = np.random.uniform(0.5, 2.0, T)
    raw = n((D, T)) / s / (u * r)
    new = np.random.permutation(idx.reshape(B, N)[:, -NEW // B:].reshape(-1))
    return {
        "qT": (n((B, D, NQ)) * s * (0.60 / np.sqrt(D))).astype(np.float32),
        "cT": np.where(np.isin(np.arange(T), new)[None, :], n((D, T)), raw).astype(np.float32),
        "new_cT": raw[:, new].astype(np.float32),
        "ts": np.tile(u * r, (128, 1)).astype(np.float32),
        "ch": np.tile(s[:, 0] * np.random.uniform(0.5, 2.0, D), (128, 1)).astype(np.float32),
        "offs": striped(idx),
        "slots": striped(new),
    }


def reference(qT, cT, new_cT, ts, ch, offs, slots):
    idx = unstriped(offs)
    c = f64(cT)
    c[:, unstriped(slots)] = f64(new_cT)
    pick = lambda x: x[:, idx].reshape(x.shape[0], B, N).transpose(1, 0, 2)
    q = f64(qT)
    score = mxq(q, 1, "e4m3").transpose(0, 2, 1) @ mxq(pick(c), 1, "e4m3")
    score = score * pick(f64(ts))[:, :1, :]
    m = score.max(-1, keepdims=True)
    p = np.exp(score - m)
    total = p.sum(-1, keepdims=True)
    w = p * pick(f64(ts))[:, :1, :]
    y = mxq(w, 2, "e4m3") @ mxq(pick(c).transpose(0, 2, 1), 1, "e4m3")
    y = y / total
    y = y * f64(ch)[:1]
    return y

@@ -1,0 +1,181 @@
+from contextlib import ExitStack
+
+import concourse.mybir as mybir
+from concourse.masks import make_identity
+
+F32 = mybir.dt.float32
+BF16 = mybir.dt.bfloat16
+U32 = mybir.dt.uint32
+U16 = mybir.dt.uint16
+U8 = mybir.dt.uint8
+FP8X4 = mybir.dt.float8_e4m3fn_x4
+MULT = mybir.AluOpType.mult
+ADD = mybir.AluOpType.add
+MAX = mybir.AluOpType.max
+AX = mybir.AxisListType
+ACT = mybir.ActivationFunctionType
+
+P = 128
+T = 1024
+NEW = 256
+N = 512
+D = 512
+NQ = 128
+HALF = 256
+
+FLOPS = 2 * NQ * N * D * 2
+
+
+def tile_attend_x_mla_append256_topk_kernel(tc, qT, cT, new_cT, ts, ch, offs, slots, out):
+    nc = tc.nc
+    with ExitStack() as ctx:
+        lists = ctx.enter_context(tc.tile_pool(name="lists", bufs=1))
+        keep = ctx.enter_context(tc.tile_pool(name="keep", bufs=1))
+        psum = ctx.enter_context(tc.psum_pool(name="psum", bufs=1))
+
+        slots_sb = lists.tile([P, NEW // 16], U16, name="slots_sb")
+        offs_sb = lists.tile([P, N // 16], U16, name="offs_sb")
+
+        new_sb = keep.tile([P, 4, NEW], F32, name="new_sb")
+        pool = [keep.tile([P, T], F32, name=f"pool{t}") for t in range(4)]
+        q_raw = keep.tile([P, 4, NQ], F32, name="q_raw")
+        ts_sb = keep.tile([P, T], F32, name="ts_sb")
+        ch_sb = keep.tile([P, D], F32, name="ch_sb")
+
+        new_view = new_cT.rearrange("(p j) w -> p j w", j=4)
+        pool_view = cT.rearrange("(p j) w -> p j w", j=4)
+
+        nc.sync.dma_start(slots_sb[:], slots)
+        nc.sync.dma_start(new_sb[:, 0, :], new_view[:, 0, :])
+        nc.sync.dma_start(pool[0][:], pool_view[:, 0, :])
+        nc.sync.dma_start(new_sb[:, 1:4, :], new_view[:, 1:4, :])
+        nc.sync.dma_start(pool[1][:], pool_view[:, 1, :])
+        nc.sync.dma_start(q_raw[:], qT[0].rearrange("(p j) w -> p j w", j=4))
+        nc.sync.dma_start(pool[2][:], pool_view[:, 2, :])
+        nc.sync.dma_start(pool[3][:], pool_view[:, 3, :])
+        nc.sync.dma_start(offs_sb[:], offs)
+        nc.sync.dma_start(ts_sb[:], ts)
+        nc.sync.dma_start(ch_sb[:], ch)
+
+        warm = keep.tile([P, 1], F32, name="warm")
+        nc.vector.memset(warm[:], 0.0)
+        warm_out = keep.tile([P, 1], F32, name="warm_out")
+        nc.scalar.activation(out=warm_out[:], in_=warm[:], func=ACT.Exp)
+
+        ident = keep.tile([P, P], F32, name="ident")
+        make_identity(nc, ident[:])
+
+        pairs = [keep.tile([P, 2 * T], BF16, name=f"pairs{u}", align_bytes=64) for u in range(2)]
+        q_bf = keep.tile([P, NQ, 4], BF16, name="q_bf", align_bytes=64)
+        q_codes = keep.tile([P, NQ], U32, name="q_codes", align_bytes=64)
+        q_scales = keep.tile([P, NQ], U8, name="q_scales", align_bytes=64)
+
+        nc.scalar.activation(out=q_bf[:], in_=q_raw[:].rearrange("p j q -> p q j"), func=ACT.Copy)
+        for t in range(4):
+            nc.vector.tensor_copy(pool[t][:].indirect(slots_sb[:]), new_sb[:, t, :])
+            nc.scalar.activation(
+                out=pairs[t // 2][:].rearrange("p (n j) -> p n j", j=2)[:, :, t % 2], in_=pool[t][:], func=ACT.Copy
+            )
+
+        latents = keep.tile([P, 4 * N], BF16, name="latents", align_bytes=64)
+        words = latents[:].bitcast(U32).rearrange("p (n u) -> p n u", u=2)
+        ts_g = keep.tile([P, N], F32, name="ts_g")
+        nc.vector.tensor_copy(words[:, :, 0], pairs[0][:].bitcast(U32).indirect(offs_sb[:]))
+        nc.vector.tensor_copy(ts_g[:], ts_sb[:].indirect(offs_sb[:]))
+        nc.vector.tensor_copy(words[:, :, 1], pairs[1][:].bitcast(U32).indirect(offs_sb[:]))
+
+        k_codes = keep.tile([P, N], U32, name="k_codes", align_bytes=64)
+        k_scales = keep.tile([P, N], U8, name="k_scales", align_bytes=64)
+        scores = psum.tile([P, N], F32, name="scores")
+        nc.vector.quantize_mx(
+            out=q_codes[:].bitcast(FP8X4), scales=q_scales[:], in_=q_bf[:].rearrange("p q j -> p (q j)")
+        )
+        for h in range(2):
+            cols = slice(h * HALF, (h + 1) * HALF)
+            nc.vector.quantize_mx(
+                out=k_codes[:, cols].bitcast(FP8X4),
+                scales=k_scales[:, cols],
+                in_=latents[:, 4 * h * HALF : 4 * (h + 1) * HALF],
+            )
+
+        turned = [psum.tile([P, 4, P], F32, name=f"turned{u}") for u in range(2)]
+        word_view = latents[:].bitcast(F32).rearrange("p (m s u) -> p s u m", s=4, u=2)
+        values = keep.tile([P, 4 * D], BF16, name="values", align_bytes=64)
+        value_view = values[:].rearrange("p (m u j s) -> p u m j s", u=2, j=2, s=4)
+        for u in range(2):
+            for s in range(4):
+                nc.tensor.transpose(turned[u][:, s, :], word_view[:, s, u, :], ident[:])
+            nc.scalar.copy(
+                value_view[:, u],
+                turned[u][:].rearrange("p s m -> p (s m)").bitcast(BF16).rearrange("p (s m j) -> p m j s", s=4, j=2),
+            )
+
+        for h in range(2):
+            cols = slice(h * HALF, (h + 1) * HALF)
+            nc.tensor.matmul_mx(
+                out=scores[:, cols],
+                lhsT=q_codes[:].bitcast(FP8X4),
+                lhsT_scale=q_scales[:],
+                rhs=k_codes[:, cols].bitcast(FP8X4),
+                rhs_scale=k_scales[:, cols],
+                start=True,
+                stop=True,
+            )
+
+        a = keep.tile([P, 2, N // 4, 2], F32, name="a")
+        for h in range(2):
+            cols = slice(h * HALF, (h + 1) * HALF)
+            nc.vector.tensor_tensor(
+                a[:, :, h * 64 : (h + 1) * 64, :].rearrange("p u m j -> p m u j"),
+                scores[:, cols].rearrange("p (m u j) -> p m u j", u=2, j=2),
+                ts_g[:, cols].rearrange("p (m u j) -> p m u j", u=2, j=2),
+                MULT,
+            )
+        neg_m = keep.tile([P, 1], F32, name="neg_m")
+        nc.vector.tensor_reduce(
+            out=neg_m[:], in_=a[:].rearrange("p u m j -> p (u m j)"), axis=AX.X, op=MAX, negate=True
+        )
+        v_codes = keep.tile([P, D], U32, name="v_codes", align_bytes=64)
+        v_scales = keep.tile([P, D], U8, name="v_scales", align_bytes=64)
+        nc.vector.quantize_mx(out=v_codes[:].bitcast(FP8X4), scales=v_scales[:], in_=values[:])
+
+        prob = keep.tile([P, 2, N // 4, 2], F32, name="prob")
+        sums = keep.tile([P, 2], F32, name="sums")
+        w = keep.tile([P, 2, N // 4, 2], BF16, name="w", align_bytes=64)
+        ts_view = ts_g[:].rearrange("p (m u j) -> p u m j", u=2, j=2)
+        w_turned = psum.tile([P, 2, P], F32, name="w_turned")
+        w_words = w[:].rearrange("p u m j -> p (u m j)").bitcast(F32)
+        for u in range(2):
+            nc.scalar.activation(
+                out=prob[:, u], in_=a[:, u], func=ACT.Exp, bias=neg_m[:], scale=1.0, accum_out=sums[:, u : u + 1]
+            )
+            nc.vector.tensor_tensor(w[:, u], prob[:, u], ts_view[:, u], MULT)
+            nc.tensor.transpose(w_turned[:, u, :], w_words[:, u * P : (u + 1) * P], ident[:])
+
+        w_grouped = keep.tile([P, 4 * NQ], BF16, name="w_grouped", align_bytes=64)
+        nc.scalar.copy(
+            w_grouped[:].bitcast(F32).rearrange("p (q u) -> p q u", u=2), w_turned[:].rearrange("p u q -> p q u")
+        )
+        total = keep.tile([P, 1], F32, name="total")
+        inv = keep.tile([P, 1], F32, name="inv")
+        nc.vector.tensor_tensor(total[:], sums[:, 0:1], sums[:, 1:2], ADD)
+        nc.vector.reciprocal(inv[:], total[:])
+        w_codes = keep.tile([P, NQ], U32, name="w_codes", align_bytes=64)
+        w_scales = keep.tile([P, NQ], U8, name="w_scales", align_bytes=64)
+        nc.vector.quantize_mx(out=w_codes[:].bitcast(FP8X4), scales=w_scales[:], in_=w_grouped[:])
+
+        y = psum.tile([P, D], F32, name="y")
+        result = keep.tile([P, D], F32, name="result")
+        for h in range(2):
+            cols = slice(h * HALF, (h + 1) * HALF)
+            nc.tensor.matmul_mx(
+                out=y[:, cols],
+                lhsT=w_codes[:].bitcast(FP8X4),
+                lhsT_scale=w_scales[:],
+                rhs=v_codes[:, cols].bitcast(FP8X4),
+                rhs_scale=v_scales[:, cols],
+                start=True,
+                stop=True,
+            )
+            nc.vector.scalar_tensor_tensor(result[:, cols], y[:, cols], inv[:], ch_sb[:, cols], MULT, MULT)
+            nc.sync.dma_start(out[0][:, cols], result[:, cols])

@@ -36,8 +36,8 @@ def tile_attend_x_mla_append256_topk_kernel(tc, qT, cT, new_cT, ts, ch, offs, sl
         slots_sb = lists.tile([P, NEW // 16], U16, name="slots_sb")
         offs_sb = lists.tile([P, N // 16], U16, name="offs_sb")
 
-        new_sb = keep.tile([P, 4, NEW], F32, name="new_sb")
-        pool = [keep.tile([P, T], F32, name=f"pool{t}") for t in range(4)]
+        new_sb = [keep.tile([P, NEW], F32, name=f"new{t}", tag=f"new{t}", align_bytes=64) for t in range(4)]
+        pool = [keep.tile([P, T], F32, name=f"pool{t}", tag=f"pool{t}", align_bytes=64) for t in range(4)]
         q_raw = keep.tile([P, 4, NQ], F32, name="q_raw")
         ts_sb = keep.tile([P, T], F32, name="ts_sb")
         ch_sb = keep.tile([P, D], F32, name="ch_sb")
@@ -46,15 +46,13 @@ def tile_attend_x_mla_append256_topk_kernel(tc, qT, cT, new_cT, ts, ch, offs, sl
         pool_view = cT.rearrange("(p j) w -> p j w", j=4)
 
         nc.sync.dma_start(slots_sb[:], slots)
-        nc.sync.dma_start(new_sb[:, 0, :], new_view[:, 0, :])
-        nc.sync.dma_start(pool[0][:], pool_view[:, 0, :])
-        nc.sync.dma_start(new_sb[:, 1:4, :], new_view[:, 1:4, :])
-        nc.sync.dma_start(pool[1][:], pool_view[:, 1, :])
-        nc.sync.dma_start(q_raw[:], qT[0].rearrange("(p j) w -> p j w", j=4))
-        nc.sync.dma_start(pool[2][:], pool_view[:, 2, :])
-        nc.sync.dma_start(pool[3][:], pool_view[:, 3, :])
-        nc.sync.dma_start(offs_sb[:], offs)
+        for t in range(4):
+            nc.sync.dma_start(new_sb[t][:], new_view[:, t, :])
+            nc.sync.dma_start(pool[t][:], pool_view[:, t, :])
+            if t == 0:
+                nc.sync.dma_start(offs_sb[:], offs)
         nc.sync.dma_start(ts_sb[:], ts)
+        nc.sync.dma_start(q_raw[:], qT[0].rearrange("(p j) w -> p j w", j=4))
         nc.sync.dma_start(ch_sb[:], ch)
 
         warm = keep.tile([P, 1], F32, name="warm")
@@ -66,23 +64,21 @@ def tile_attend_x_mla_append256_topk_kernel(tc, qT, cT, new_cT, ts, ch, offs, sl
         make_identity(nc, ident[:])
 
         pairs = [keep.tile([P, 2 * T], BF16, name=f"pairs{u}", align_bytes=64) for u in range(2)]
-        q_bf = keep.tile([P, NQ, 4], BF16, name="q_bf", align_bytes=64)
+        SHARE = 640
+        for t in range(4):
+            nc.vector.tensor_copy(pool[t][:].indirect(slots_sb[:]), new_sb[t][:])
+            place = pairs[t // 2][:].rearrange("p (n j) -> p n j", j=2)[:, :, t % 2]
+            nc.scalar.activation(out=place[:, 0:SHARE], in_=pool[t][:, 0:SHARE], func=ACT.Copy)
+            nc.gpsimd.tensor_copy(place[:, SHARE:T], pool[t][:, SHARE:T])
+        q_bf = keep.tile([P, NQ, 4], BF16, name="q_bf", tag="pool3", align_bytes=64)
         q_codes = keep.tile([P, NQ], U32, name="q_codes", align_bytes=64)
         q_scales = keep.tile([P, NQ], U8, name="q_scales", align_bytes=64)
+        nc.gpsimd.tensor_copy(q_bf[:], q_raw[:].rearrange("p j q -> p q j"))
 
-        nc.scalar.activation(out=q_bf[:], in_=q_raw[:].rearrange("p j q -> p q j"), func=ACT.Copy)
-        for t in range(4):
-            nc.vector.tensor_copy(pool[t][:].indirect(slots_sb[:]), new_sb[:, t, :])
-            nc.scalar.activation(
-                out=pairs[t // 2][:].rearrange("p (n j) -> p n j", j=2)[:, :, t % 2], in_=pool[t][:], func=ACT.Copy
-            )
-
-        latents = keep.tile([P, 4 * N], BF16, name="latents", align_bytes=64)
+        latents = keep.tile([P, 4 * N], BF16, name="latents", tag="new3", align_bytes=64)
         words = latents[:].bitcast(U32).rearrange("p (n u) -> p n u", u=2)
-        ts_g = keep.tile([P, N], F32, name="ts_g")
-        nc.vector.tensor_copy(words[:, :, 0], pairs[0][:].bitcast(U32).indirect(offs_sb[:]))
-        nc.vector.tensor_copy(ts_g[:], ts_sb[:].indirect(offs_sb[:]))
-        nc.vector.tensor_copy(words[:, :, 1], pairs[1][:].bitcast(U32).indirect(offs_sb[:]))
+        for u in range(2):
+            nc.vector.tensor_copy(words[:, :, u], pairs[u][:].bitcast(U32).indirect(offs_sb[:]))
 
         k_codes = keep.tile([P, N], U32, name="k_codes", align_bytes=64)
         k_scales = keep.tile([P, N], U8, name="k_scales", align_bytes=64)
@@ -98,6 +94,9 @@ def tile_attend_x_mla_append256_topk_kernel(tc, qT, cT, new_cT, ts, ch, offs, sl
                 in_=latents[:, 4 * h * HALF : 4 * (h + 1) * HALF],
             )
 
+        ts_g = keep.tile([P, N], F32, name="ts_g", tag="pool3", align_bytes=64)
+        nc.vector.tensor_copy(ts_g[:], ts_sb[:].indirect(offs_sb[:]))
+
         turned = [psum.tile([P, 4, P], F32, name=f"turned{u}") for u in range(2)]
         word_view = latents[:].bitcast(F32).rearrange("p (m s u) -> p s u m", s=4, u=2)
         values = keep.tile([P, 4 * D], BF16, name="values", align_bytes=64)
@@ -110,6 +109,8 @@ def tile_attend_x_mla_append256_topk_kernel(tc, qT, cT, new_cT, ts, ch, offs, sl
                 turned[u][:].rearrange("p s m -> p (s m)").bitcast(BF16).rearrange("p (s m j) -> p m j s", s=4, j=2),
             )
 
+        a = keep.tile([P, N], F32, name="a")
+        neg_m = keep.tile([P, 1], F32, name="neg_m")
         for h in range(2):
             cols = slice(h * HALF, (h + 1) * HALF)
             nc.tensor.matmul_mx(
@@ -121,20 +122,9 @@ def tile_attend_x_mla_append256_topk_kernel(tc, qT, cT, new_cT, ts, ch, offs, sl
                 start=True,
                 stop=True,
             )
+            nc.vector.tensor_tensor(a[:, cols], scores[:, cols], ts_g[:, cols], MULT)
+        nc.vector.tensor_reduce(out=neg_m[:], in_=a[:], axis=AX.X, op=MAX, negate=True)
 
-        a = keep.tile([P, 2, N // 4, 2], F32, name="a")
-        for h in range(2):
-            cols = slice(h * HALF, (h + 1) * HALF)
-            nc.vector.tensor_tensor(
-                a[:, :, h * 64 : (h + 1) * 64, :].rearrange("p u m j -> p m u j"),
-                scores[:, cols].rearrange("p (m u j) -> p m u j", u=2, j=2),
-                ts_g[:, cols].rearrange("p (m u j) -> p m u j", u=2, j=2),
-                MULT,
-            )
-        neg_m = keep.tile([P, 1], F32, name="neg_m")
-        nc.vector.tensor_reduce(
-            out=neg_m[:], in_=a[:].rearrange("p u m j -> p (u m j)"), axis=AX.X, op=MAX, negate=True
-        )
         v_codes = keep.tile([P, D], U32, name="v_codes", align_bytes=64)
         v_scales = keep.tile([P, D], U8, name="v_scales", align_bytes=64)
         nc.vector.quantize_mx(out=v_codes[:].bitcast(FP8X4), scales=v_scales[:], in_=values[:])
@@ -142,12 +132,13 @@ def tile_attend_x_mla_append256_topk_kernel(tc, qT, cT, new_cT, ts, ch, offs, sl
         prob = keep.tile([P, 2, N // 4, 2], F32, name="prob")
         sums = keep.tile([P, 2], F32, name="sums")
         w = keep.tile([P, 2, N // 4, 2], BF16, name="w", align_bytes=64)
+        a_view = a[:].rearrange("p (m u j) -> p u m j", u=2, j=2)
         ts_view = ts_g[:].rearrange("p (m u j) -> p u m j", u=2, j=2)
         w_turned = psum.tile([P, 2, P], F32, name="w_turned")
         w_words = w[:].rearrange("p u m j -> p (u m j)").bitcast(F32)
         for u in range(2):
             nc.scalar.activation(
-                out=prob[:, u], in_=a[:, u], func=ACT.Exp, bias=neg_m[:], scale=1.0, accum_out=sums[:, u : u + 1]
+                out=prob[:, u], in_=a_view[:, u], func=ACT.Exp, bias=neg_m[:], scale=1.0, accum_out=sums[:, u : u + 1]
             )
             nc.vector.tensor_tensor(w[:, u], prob[:, u], ts_view[:, u], MULT)
             nc.tensor.transpose(w_turned[:, u, :], w_words[:, u * P : (u + 1) * P], ident[:])

@@ -75,10 +75,15 @@ def tile_attend_x_mla_append256_topk_kernel(tc, qT, cT, new_cT, ts, ch, offs, sl
         q_scales = keep.tile([P, NQ], U8, name="q_scales", align_bytes=64)
         nc.gpsimd.tensor_copy(q_bf[:], q_raw[:].rearrange("p j q -> p q j"))
 
-        latents = keep.tile([P, 4 * N], BF16, name="latents", tag="new3", align_bytes=64)
+        latents = keep.tile([P, 4 * N], BF16, name="latents", align_bytes=64)
         words = latents[:].bitcast(U32).rearrange("p (n u) -> p n u", u=2)
-        for u in range(2):
-            nc.vector.tensor_copy(words[:, :, u], pairs[u][:].bitcast(U32).indirect(offs_sb[:]))
+        words0 = keep.tile([P, N], U32, name="words0", tag="new3", align_bytes=64)
+        nc.vector.tensor_copy(words0[:], pairs[0][:].bitcast(U32).indirect(offs_sb[:]))
+        nc.scalar.copy(
+            latents[:].rearrange("p (n u j) -> p n u j", u=2, j=2)[:, :, 0, :],
+            words0[:].bitcast(BF16).rearrange("p (n j) -> p n j", j=2),
+        )
+        nc.vector.tensor_copy(words[:, :, 1], pairs[1][:].bitcast(U32).indirect(offs_sb[:]))
 
         k_codes = keep.tile([P, N], U32, name="k_codes", align_bytes=64)
         k_scales = keep.tile([P, N], U8, name="k_scales", align_bytes=64)
@@ -86,48 +91,52 @@ def tile_attend_x_mla_append256_topk_kernel(tc, qT, cT, new_cT, ts, ch, offs, sl
         nc.vector.quantize_mx(
             out=q_codes[:].bitcast(FP8X4), scales=q_scales[:], in_=q_bf[:].rearrange("p q j -> p (q j)")
         )
-        for h in range(2):
-            cols = slice(h * HALF, (h + 1) * HALF)
-            nc.vector.quantize_mx(
-                out=k_codes[:, cols].bitcast(FP8X4),
-                scales=k_scales[:, cols],
-                in_=latents[:, 4 * h * HALF : 4 * (h + 1) * HALF],
-            )
+        nc.vector.quantize_mx(out=k_codes[:].bitcast(FP8X4), scales=k_scales[:], in_=latents[:])
 
         ts_g = keep.tile([P, N], F32, name="ts_g", tag="pool3", align_bytes=64)
         nc.vector.tensor_copy(ts_g[:], ts_sb[:].indirect(offs_sb[:]))
 
         turned = [psum.tile([P, 4, P], F32, name=f"turned{u}") for u in range(2)]
-        word_view = latents[:].bitcast(F32).rearrange("p (m s u) -> p s u m", s=4, u=2)
+        word_views = [
+            words0[:].bitcast(F32).rearrange("p (m s) -> p s m", s=4),
+            latents[:].bitcast(F32).rearrange("p (m s u) -> p u s m", s=4, u=2)[:, 1],
+        ]
         values = keep.tile([P, 4 * D], BF16, name="values", align_bytes=64)
         value_view = values[:].rearrange("p (m u j s) -> p u m j s", u=2, j=2, s=4)
         for u in range(2):
             for s in range(4):
-                nc.tensor.transpose(turned[u][:, s, :], word_view[:, s, u, :], ident[:])
-            nc.scalar.copy(
-                value_view[:, u],
-                turned[u][:].rearrange("p s m -> p (s m)").bitcast(BF16).rearrange("p (s m j) -> p m j s", s=4, j=2),
-            )
+                nc.tensor.transpose(turned[u][:, s, :], word_views[u][:, s, :], ident[:])
+        for h in range(2):
+            part = slice(h * 64, (h + 1) * 64)
+            for u in range(2):
+                bank = turned[u][:].rearrange("p s m -> p (s m)").bitcast(BF16)
+                nc.scalar.copy(
+                    value_view[:, u, part], bank.rearrange("p (s m j) -> p m j s", s=4, j=2)[:, part]
+                )
 
         a = keep.tile([P, N], F32, name="a")
         neg_m = keep.tile([P, 1], F32, name="neg_m")
-        for h in range(2):
-            cols = slice(h * HALF, (h + 1) * HALF)
-            nc.tensor.matmul_mx(
-                out=scores[:, cols],
-                lhsT=q_codes[:].bitcast(FP8X4),
-                lhsT_scale=q_scales[:],
-                rhs=k_codes[:, cols].bitcast(FP8X4),
-                rhs_scale=k_scales[:, cols],
-                start=True,
-                stop=True,
-            )
-            nc.vector.tensor_tensor(a[:, cols], scores[:, cols], ts_g[:, cols], MULT)
+        nc.tensor.matmul_mx(
+            out=scores[:],
+            lhsT=q_codes[:].bitcast(FP8X4),
+            lhsT_scale=q_scales[:],
+            rhs=k_codes[:].bitcast(FP8X4),
+            rhs_scale=k_scales[:],
+            start=True,
+            stop=True,
+        )
+        nc.vector.tensor_tensor(a[:], scores[:], ts_g[:], MULT)
         nc.vector.tensor_reduce(out=neg_m[:], in_=a[:], axis=AX.X, op=MAX, negate=True)
 
         v_codes = keep.tile([P, D], U32, name="v_codes", align_bytes=64)
         v_scales = keep.tile([P, D], U8, name="v_scales", align_bytes=64)
-        nc.vector.quantize_mx(out=v_codes[:].bitcast(FP8X4), scales=v_scales[:], in_=values[:])
+        for h in range(2):
+            cols = slice(h * HALF, (h + 1) * HALF)
+            nc.vector.quantize_mx(
+                out=v_codes[:, cols].bitcast(FP8X4),
+                scales=v_scales[:, cols],
+                in_=values[:, 4 * h * HALF : 4 * (h + 1) * HALF],
+            )
 
         prob = keep.tile([P, 2, N // 4, 2], F32, name="prob")
         sums = keep.tile([P, 2], F32, name="sums")
@@ -157,16 +166,16 @@ def tile_attend_x_mla_append256_topk_kernel(tc, qT, cT, new_cT, ts, ch, offs, sl
 
         y = psum.tile([P, D], F32, name="y")
         result = keep.tile([P, D], F32, name="result")
+        nc.tensor.matmul_mx(
+            out=y[:],
+            lhsT=w_codes[:].bitcast(FP8X4),
+            lhsT_scale=w_scales[:],
+            rhs=v_codes[:].bitcast(FP8X4),
+            rhs_scale=v_scales[:],
+            start=True,
+            stop=True,
+        )
         for h in range(2):
             cols = slice(h * HALF, (h + 1) * HALF)
-            nc.tensor.matmul_mx(
-                out=y[:, cols],
-                lhsT=w_codes[:].bitcast(FP8X4),
-                lhsT_scale=w_scales[:],
-                rhs=v_codes[:, cols].bitcast(FP8X4),
-                rhs_scale=v_scales[:, cols],
-                start=True,
-                stop=True,
-            )
             nc.vector.scalar_tensor_tensor(result[:, cols], y[:, cols], inv[:], ch_sb[:, cols], MULT, MULT)
             nc.sync.dma_start(out[0][:, cols], result[:, cols])

@@ -36,7 +36,9 @@ def tile_attend_x_mla_append256_topk_kernel(tc, qT, cT, new_cT, ts, ch, offs, sl
         slots_sb = lists.tile([P, NEW // 16], U16, name="slots_sb")
         offs_sb = lists.tile([P, N // 16], U16, name="offs_sb")
 
-        new_sb = [keep.tile([P, NEW], F32, name=f"new{t}", tag=f"new{t}", align_bytes=64) for t in range(4)]
+        new01 = [keep.tile([P, NEW], F32, name=f"new{t}") for t in range(2)]
+        new23 = keep.tile([P, 2, NEW], F32, name="new23", tag="new23", align_bytes=64)
+        new_sb = [new01[0][:], new01[1][:], new23[:, 0, :], new23[:, 1, :]]
         pool = [keep.tile([P, T], F32, name=f"pool{t}", tag=f"pool{t}", align_bytes=64) for t in range(4)]
         q_raw = keep.tile([P, 4, NQ], F32, name="q_raw")
         ts_sb = keep.tile([P, T], F32, name="ts_sb")
@@ -47,7 +49,10 @@ def tile_attend_x_mla_append256_topk_kernel(tc, qT, cT, new_cT, ts, ch, offs, sl
 
         nc.sync.dma_start(slots_sb[:], slots)
         for t in range(4):
-            nc.sync.dma_start(new_sb[t][:], new_view[:, t, :])
+            if t < 2:
+                nc.sync.dma_start(new_sb[t], new_view[:, t, :])
+            elif t == 2:
+                nc.sync.dma_start(new23[:], new_view[:, 2:4, :])
             nc.sync.dma_start(pool[t][:], pool_view[:, t, :])
             if t == 0:
                 nc.sync.dma_start(offs_sb[:], offs)
@@ -64,12 +69,13 @@ def tile_attend_x_mla_append256_topk_kernel(tc, qT, cT, new_cT, ts, ch, offs, sl
         make_identity(nc, ident[:])
 
         pairs = [keep.tile([P, 2 * T], BF16, name=f"pairs{u}", align_bytes=64) for u in range(2)]
-        SHARE = 640
         for t in range(4):
-            nc.vector.tensor_copy(pool[t][:].indirect(slots_sb[:]), new_sb[t][:])
+            nc.vector.tensor_copy(pool[t][:].indirect(slots_sb[:]), new_sb[t])
             place = pairs[t // 2][:].rearrange("p (n j) -> p n j", j=2)[:, :, t % 2]
-            nc.scalar.activation(out=place[:, 0:SHARE], in_=pool[t][:, 0:SHARE], func=ACT.Copy)
-            nc.gpsimd.tensor_copy(place[:, SHARE:T], pool[t][:, SHARE:T])
+            share = T if t < 2 else 704
+            nc.scalar.activation(out=place[:, 0:share], in_=pool[t][:, 0:share], func=ACT.Copy)
+            if share < T:
+                nc.gpsimd.tensor_copy(place[:, share:T], pool[t][:, share:T])
         q_bf = keep.tile([P, NQ, 4], BF16, name="q_bf", tag="pool3", align_bytes=64)
         q_codes = keep.tile([P, NQ], U32, name="q_codes", align_bytes=64)
         q_scales = keep.tile([P, NQ], U8, name="q_scales", align_bytes=64)
@@ -77,7 +83,7 @@ def tile_attend_x_mla_append256_topk_kernel(tc, qT, cT, new_cT, ts, ch, offs, sl
 
         latents = keep.tile([P, 4 * N], BF16, name="latents", align_bytes=64)
         words = latents[:].bitcast(U32).rearrange("p (n u) -> p n u", u=2)
-        words0 = keep.tile([P, N], U32, name="words0", tag="new3", align_bytes=64)
+        words0 = keep.tile([P, N], U32, name="words0", tag="new23", align_bytes=64)
         nc.vector.tensor_copy(words0[:], pairs[0][:].bitcast(U32).indirect(offs_sb[:]))
         nc.scalar.copy(
             latents[:].rearrange("p (n u j) -> p n u j", u=2, j=2)[:, :, 0, :],
@@ -164,18 +170,18 @@ def tile_attend_x_mla_append256_topk_kernel(tc, qT, cT, new_cT, ts, ch, offs, sl
         w_scales = keep.tile([P, NQ], U8, name="w_scales", align_bytes=64)
         nc.vector.quantize_mx(out=w_codes[:].bitcast(FP8X4), scales=w_scales[:], in_=w_grouped[:])
 
-        y = psum.tile([P, D], F32, name="y")
+        y = [psum.tile([P, HALF], F32, name=f"y{h}") for h in range(2)]
         result = keep.tile([P, D], F32, name="result")
-        nc.tensor.matmul_mx(
-            out=y[:],
-            lhsT=w_codes[:].bitcast(FP8X4),
-            lhsT_scale=w_scales[:],
-            rhs=v_codes[:].bitcast(FP8X4),
-            rhs_scale=v_scales[:],
-            start=True,
-            stop=True,
-        )
         for h in range(2):
             cols = slice(h * HALF, (h + 1) * HALF)
-            nc.vector.scalar_tensor_tensor(result[:, cols], y[:, cols], inv[:], ch_sb[:, cols], MULT, MULT)
+            nc.tensor.matmul_mx(
+                out=y[h][:],
+                lhsT=w_codes[:].bitcast(FP8X4),
+                lhsT_scale=w_scales[:],
+                rhs=v_codes[:, cols].bitcast(FP8X4),
+                rhs_scale=v_scales[:, cols],
+                start=True,
+                stop=True,
+            )
+            nc.vector.scalar_tensor_tensor(result[:, cols], y[h][:], inv[:], ch_sb[:, cols], MULT, MULT)
             nc.sync.dma_start(out[0][:, cols], result[:, cols])

from contextlib import ExitStack

import concourse.mybir as mybir
from concourse.masks import make_identity

F32 = mybir.dt.float32
BF16 = mybir.dt.bfloat16
U32 = mybir.dt.uint32
U16 = mybir.dt.uint16
U8 = mybir.dt.uint8
FP8X4 = mybir.dt.float8_e4m3fn_x4
MULT = mybir.AluOpType.mult
ADD = mybir.AluOpType.add
MAX = mybir.AluOpType.max
AX = mybir.AxisListType
ACT = mybir.ActivationFunctionType

P = 128
T = 1024
NEW = 256
N = 512
D = 512
NQ = 128
HALF = 256

FLOPS = 2 * NQ * N * D * 2


def tile_attend_x_mla_append256_topk_kernel(tc, qT, cT, new_cT, ts, ch, offs, slots, out):
    nc = tc.nc
    with ExitStack() as ctx:
        lists = ctx.enter_context(tc.tile_pool(name="lists", bufs=1))
        keep = ctx.enter_context(tc.tile_pool(name="keep", bufs=1))
        psum = ctx.enter_context(tc.psum_pool(name="psum", bufs=1))

        slots_sb = lists.tile([P, NEW // 16], U16, name="slots_sb")
        offs_sb = lists.tile([P, N // 16], U16, name="offs_sb")

        new01 = [keep.tile([P, NEW], F32, name=f"new{t}") for t in range(2)]
        new23 = keep.tile([P, 2, NEW], F32, name="new23", tag="new23", align_bytes=64)
        new_sb = [new01[0][:], new01[1][:], new23[:, 0, :], new23[:, 1, :]]
        pool = [keep.tile([P, T], F32, name=f"pool{t}", tag=f"pool{t}", align_bytes=64) for t in range(4)]
        q_raw = keep.tile([P, 4, NQ], F32, name="q_raw")
        ts_sb = keep.tile([P, T], F32, name="ts_sb")
        ch_sb = keep.tile([P, D], F32, name="ch_sb")

        new_view = new_cT.rearrange("(p j) w -> p j w", j=4)
        pool_view = cT.rearrange("(p j) w -> p j w", j=4)

        nc.sync.dma_start(slots_sb[:], slots)
        for t in range(4):
            if t < 2:
                nc.sync.dma_start(new_sb[t], new_view[:, t, :])
            elif t == 2:
                nc.sync.dma_start(new23[:], new_view[:, 2:4, :])
            nc.sync.dma_start(pool[t][:], pool_view[:, t, :])
            if t == 0:
                nc.sync.dma_start(offs_sb[:], offs)
        nc.sync.dma_start(ts_sb[:], ts)
        nc.sync.dma_start(q_raw[:], qT[0].rearrange("(p j) w -> p j w", j=4))
        nc.sync.dma_start(ch_sb[:], ch)

        warm = keep.tile([P, 1], F32, name="warm")
        nc.vector.memset(warm[:], 0.0)
        warm_out = keep.tile([P, 1], F32, name="warm_out")
        nc.scalar.activation(out=warm_out[:], in_=warm[:], func=ACT.Exp)

        ident = keep.tile([P, P], F32, name="ident")
        make_identity(nc, ident[:])

        pairs = [keep.tile([P, 2 * T], BF16, name=f"pairs{u}", align_bytes=64) for u in range(2)]
        for t in range(4):
            nc.vector.tensor_copy(pool[t][:].indirect(slots_sb[:]), new_sb[t])
            place = pairs[t // 2][:].rearrange("p (n j) -> p n j", j=2)[:, :, t % 2]
            share = T if t < 2 else 704
            nc.scalar.activation(out=place[:, 0:share], in_=pool[t][:, 0:share], func=ACT.Copy)
            if share < T:
                nc.gpsimd.tensor_copy(place[:, share:T], pool[t][:, share:T])
        q_bf = keep.tile([P, NQ, 4], BF16, name="q_bf", tag="pool3", align_bytes=64)
        q_codes = keep.tile([P, NQ], U32, name="q_codes", align_bytes=64)
        q_scales = keep.tile([P, NQ], U8, name="q_scales", align_bytes=64)
        nc.gpsimd.tensor_copy(q_bf[:], q_raw[:].rearrange("p j q -> p q j"))

        latents = keep.tile([P, 4 * N], BF16, name="latents", align_bytes=64)
        words = latents[:].bitcast(U32).rearrange("p (n u) -> p n u", u=2)
        words0 = keep.tile([P, N], U32, name="words0", tag="new23", align_bytes=64)
        nc.vector.tensor_copy(words0[:], pairs[0][:].bitcast(U32).indirect(offs_sb[:]))
        nc.scalar.copy(
            latents[:].rearrange("p (n u j) -> p n u j", u=2, j=2)[:, :, 0, :],
            words0[:].bitcast(BF16).rearrange("p (n j) -> p n j", j=2),
        )
        nc.vector.tensor_copy(words[:, :, 1], pairs[1][:].bitcast(U32).indirect(offs_sb[:]))

        k_codes = keep.tile([P, N], U32, name="k_codes", align_bytes=64)
        k_scales = keep.tile([P, N], U8, name="k_scales", align_bytes=64)
        scores = psum.tile([P, N], F32, name="scores")
        nc.vector.quantize_mx(
            out=q_codes[:].bitcast(FP8X4), scales=q_scales[:], in_=q_bf[:].rearrange("p q j -> p (q j)")
        )
        nc.vector.quantize_mx(out=k_codes[:].bitcast(FP8X4), scales=k_scales[:], in_=latents[:])

        ts_g = keep.tile([P, N], F32, name="ts_g", tag="pool3", align_bytes=64)
        nc.vector.tensor_copy(ts_g[:], ts_sb[:].indirect(offs_sb[:]))

        turned = [psum.tile([P, 4, P], F32, name=f"turned{u}") for u in range(2)]
        word_views = [
            words0[:].bitcast(F32).rearrange("p (m s) -> p s m", s=4),
            latents[:].bitcast(F32).rearrange("p (m s u) -> p u s m", s=4, u=2)[:, 1],
        ]
        values = keep.tile([P, 4 * D], BF16, name="values", align_bytes=64)
        value_view = values[:].rearrange("p (m u j s) -> p u m j s", u=2, j=2, s=4)
        for u in range(2):
            for s in range(4):
                nc.tensor.transpose(turned[u][:, s, :], word_views[u][:, s, :], ident[:])
        for h in range(2):
            part = slice(h * 64, (h + 1) * 64)
            for u in range(2):
                bank = turned[u][:].rearrange("p s m -> p (s m)").bitcast(BF16)
                nc.scalar.copy(
                    value_view[:, u, part], bank.rearrange("p (s m j) -> p m j s", s=4, j=2)[:, part]
                )

        a = keep.tile([P, N], F32, name="a")
        neg_m = keep.tile([P, 1], F32, name="neg_m")
        nc.tensor.matmul_mx(
            out=scores[:],
            lhsT=q_codes[:].bitcast(FP8X4),
            lhsT_scale=q_scales[:],
            rhs=k_codes[:].bitcast(FP8X4),
            rhs_scale=k_scales[:],
            start=True,
            stop=True,
        )
        nc.vector.tensor_tensor(a[:], scores[:], ts_g[:], MULT)
        nc.vector.tensor_reduce(out=neg_m[:], in_=a[:], axis=AX.X, op=MAX, negate=True)

        v_codes = keep.tile([P, D], U32, name="v_codes", align_bytes=64)
        v_scales = keep.tile([P, D], U8, name="v_scales", align_bytes=64)
        for h in range(2):
            cols = slice(h * HALF, (h + 1) * HALF)
            nc.vector.quantize_mx(
                out=v_codes[:, cols].bitcast(FP8X4),
                scales=v_scales[:, cols],
                in_=values[:, 4 * h * HALF : 4 * (h + 1) * HALF],
            )

        prob = keep.tile([P, 2, N // 4, 2], F32, name="prob")
        sums = keep.tile([P, 2], F32, name="sums")
        w = keep.tile([P, 2, N // 4, 2], BF16, name="w", align_bytes=64)
        a_view = a[:].rearrange("p (m u j) -> p u m j", u=2, j=2)
        ts_view = ts_g[:].rearrange("p (m u j) -> p u m j", u=2, j=2)
        w_turned = psum.tile([P, 2, P], F32, name="w_turned")
        w_words = w[:].rearrange("p u m j -> p (u m j)").bitcast(F32)
        for u in range(2):
            nc.scalar.activation(
                out=prob[:, u], in_=a_view[:, u], func=ACT.Exp, bias=neg_m[:], scale=1.0, accum_out=sums[:, u : u + 1]
            )
            nc.vector.tensor_tensor(w[:, u], prob[:, u], ts_view[:, u], MULT)
            nc.tensor.transpose(w_turned[:, u, :], w_words[:, u * P : (u + 1) * P], ident[:])

        w_grouped = keep.tile([P, 4 * NQ], BF16, name="w_grouped", align_bytes=64)
        nc.scalar.copy(
            w_grouped[:].bitcast(F32).rearrange("p (q u) -> p q u", u=2), w_turned[:].rearrange("p u q -> p q u")
        )
        total = keep.tile([P, 1], F32, name="total")
        inv = keep.tile([P, 1], F32, name="inv")
        nc.vector.tensor_tensor(total[:], sums[:, 0:1], sums[:, 1:2], ADD)
        nc.vector.reciprocal(inv[:], total[:])
        w_codes = keep.tile([P, NQ], U32, name="w_codes", align_bytes=64)
        w_scales = keep.tile([P, NQ], U8, name="w_scales", align_bytes=64)
        nc.vector.quantize_mx(out=w_codes[:].bitcast(FP8X4), scales=w_scales[:], in_=w_grouped[:])

        y = [psum.tile([P, HALF], F32, name=f"y{h}") for h in range(2)]
        result = keep.tile([P, D], F32, name="result")
        for h in range(2):
            cols = slice(h * HALF, (h + 1) * HALF)
            nc.tensor.matmul_mx(
                out=y[h][:],
                lhsT=w_codes[:].bitcast(FP8X4),
                lhsT_scale=w_scales[:],
                rhs=v_codes[:, cols].bitcast(FP8X4),
                rhs_scale=v_scales[:, cols],
                start=True,
                stop=True,
            )
            nc.vector.scalar_tensor_tensor(result[:, cols], y[h][:], inv[:], ch_sb[:, cols], MULT, MULT)
            nc.sync.dma_start(out[0][:, cols], result[:, cols])
